import numpy as np, ml_dtypes
CORES = [4,20,60,84,92,100,116]
N = 7
S, B = 2, 512
def setup_inputs(rng):
    a = (rng.standard_normal((128, 128), dtype=np.float32) / 8).astype(ml_dtypes.bfloat16)
    return {"x": (rng.standard_normal((N, 128, S * B), dtype=np.float32) / 2).astype(ml_dtypes.bfloat16), "a": np.broadcast_to(a, (N, 128, 128)).copy()}
def reference(x, a):
    X, A = x.astype(np.float64), a.astype(np.float64)
    y = np.zeros((N, 128, S * B)); h = np.zeros((128, B))
    for r in range(N):
        for s in range(S):
            h = np.tanh(A[r].T @ h + X[r][:, B * s:B * s + B])
            y[r][:, B * s:B * s + B] = h
    return {"y": y.astype(ml_dtypes.bfloat16)}

@@ -1,0 +1,225 @@
+from concourse.bass import DstId, RemoteDMATransfer
+from concourse.mybir import AluOpType, ActivationFunctionType
+
+N, S, B = 7, 2, 512
+NT = N * S
+W = 4
+C = B // W
+NBANK = 4
+NAT = (5, 6)
+
+SCRATCH = {
+    "xs": ("sbuf", [128, W, S, C], "bfloat16"),
+    "xn": ("sbuf", [128, S * B], "bfloat16"),
+    "asb": ("sbuf", [128, 128], "bfloat16"),
+    "rb": ("sbuf", [128, 2 * C], "bfloat16"),
+    "xw": ("sbuf", [128, NT, C], "bfloat16"),
+    "hb": ("sbuf", [128, NT, C], "bfloat16"),
+    "ones": ("sbuf", [128, 128], "bfloat16"),
+    "ident": ("sbuf", [128, 128], "bfloat16"),
+    "ps": ("psum", [128, NBANK * 512], "float32"),
+    "yl": ("sbuf", [128, W, S, C], "bfloat16"),
+    "yn": ("sbuf", [128, S * B], "bfloat16"),
+}
+SEMAPHORES = (["ld", "lda", "asem", "one", "idn", "snt", "rin", "yp", "y0", "y1", "st"]
+              + ["x%d" % t for t in range(NT)] + ["m%d" % t for t in range(NT)] + ["h%d" % t for t in range(NT)])
+
+
+def _bits(mask):
+    return [i for i in range(16) if (mask >> i) & 1]
+
+
+def _groups(topo, src, dsts, n):
+    m = topo.mask(src, dsts[0])
+    for d in dsts[1:]:
+        m &= topo.mask(src, d)
+    e = _bits(m)
+    k = len(e) // n
+    return [sum(1 << b for b in e[i * k:(i + 1) * k]) for i in range(n)], k
+
+
+def _plan(T, topo):
+    ranks = list(T.cores)
+    chips = [topo.chip(c) for c in ranks]
+
+    def near(a, b):
+        return a == b or topo.same_plane(a, b)
+    best = max(chips, key=lambda c: sum(1 for d in chips if near(c, d)))
+    main = [r for r in range(N) if near(chips[r], best)]
+    far = [r for r in range(N) if r not in main]
+    allc = list(range(topo.CHIPS * topo.CORES_PER_CHIP))
+    free = [c for c in range(topo.CHIPS) if near(c, best) and c not in chips]
+    wchips = (free + [chips[r] for r in main])[:W]
+    die0 = topo.die(ranks[0])
+    workers = []
+    for w, ch in enumerate(wchips):
+        cand = [c for c in allc if topo.chip(c) == ch and c not in ranks
+                and all(topo.may_write(c, q) for q in ranks)]
+        want = [c for c in cand if (topo.die(c) == die0) == (w % 2 == 0)]
+        workers.append((want or cand)[0])
+    relays = {}
+    for r in far:
+        relays[r] = [c for c in allc if topo.chip(c) == chips[r] and c != ranks[r]
+                     and all(topo.may_write(c, q) for q in workers)][:4]
+    asend = {main[-1]: workers[:W // 2], main[-2]: workers[W // 2:]}
+    return ranks, main, far, workers, relays, asend
+
+
+def _dst(topo, c):
+    rid, pid, _ = topo.addr(c)
+    return DstId(rid=rid, pnc=pid)
+
+
+def _rank(g, core, T, topo, r, plan):
+    ranks, main, far, workers, relays, asend = plan
+    sem = T.sem
+    sent = 0
+    if r in main:
+        if r in asend:
+            g.scalar.dma_start(T.asb[:], T.a[:]).then_inc(sem.lda, 16)
+        g.sync.dma_start(T.xs[:, :, 0, :], T.x[:, 0:B]).then_inc(sem.ld, 16)
+        g.scalar.dma_start(T.xs[:, :, 1, :], T.x[:, B:2 * B]).then_inc(sem.ld, 16)
+        if r in asend:
+            to = asend[r]
+            ms, k = _groups(topo, core, workers, len(to))
+            g.wait_ge(sem.lda, 16)
+            g.remote_dma_fused([RemoteDMATransfer(dst_ids=[_dst(topo, d)], dma_engine_mask=ms[i], remote_sem=sem.asem,
+                                                  src=T.asb[:], dst=T.asb[:]) for i, d in enumerate(to)],
+                               local_sem=sem.snt)
+            sent += k * len(to)
+        ms, k = _groups(topo, core, workers, W)
+        g.wait_ge(sem.ld, 32)
+        g.remote_dma_fused([RemoteDMATransfer(dst_ids=[_dst(topo, d)], dma_engine_mask=ms[w],
+                                              remote_sem=sem["x%d" % (S * r)],
+                                              src=T.xs[:, w, :, :], dst=T.xw[:, S * r:S * r + S, :])
+                            for w, d in enumerate(workers)], local_sem=sem.snt)
+        sent += k * W
+    else:
+        rl = relays[r]
+        g.sync.dma_start(T.xn[:], T.x[:]).then_inc(sem.ld, 16)
+        ms, k = _groups(topo, core, rl, 4)
+        g.wait_ge(sem.ld, 16)
+        g.remote_dma_fused([RemoteDMATransfer(dst_ids=[_dst(topo, d)], dma_engine_mask=ms[q], remote_sem=sem.rin,
+                                              src=T.xn[:, q * 2 * C:(q + 1) * 2 * C], dst=T.rb[:])
+                            for q, d in enumerate(rl)], local_sem=sem.snt)
+        sent += k * 4
+    full = sum(_back_engines(topo, d, core)[1] for d in workers)
+    if r in NAT:
+        g.sync.wait_ge(sem.y0, full)
+        g.sync.dma_start(T.y[:, 0:B], T.yn[:, 0:B]).then_inc(sem.st, 16)
+        g.scalar.wait_ge(sem.y1, full)
+        g.scalar.dma_start(T.y[:, B:2 * B], T.yn[:, B:2 * B]).then_inc(sem.st, 16)
+    else:
+        g.sync.wait_ge(sem.yp, full)
+        g.sync.dma_start(T.y[:, 0:B], T.yl[:, :, 0, :]).then_inc(sem.st, 16)
+        g.scalar.wait_ge(sem.yp, full)
+        g.scalar.dma_start(T.y[:, B:2 * B], T.yl[:, :, 1, :]).then_inc(sem.st, 16)
+    g.wait_ge(sem.snt, sent)
+    g.wait_ge(sem.st, 32)
+
+
+def _back_engines(topo, worker, rank_core):
+    e = _bits(topo.mask(worker, rank_core))[:8]
+    return sum(1 << b for b in e), len(e)
+
+
+def _relay(g, core, T, topo, r, q, plan):
+    workers = plan[3]
+    sem = T.sem
+    s, hf = q // 2, q % 2
+    t = S * r + s
+    to = [workers[2 * hf], workers[2 * hf + 1]]
+    _, kin = _groups(topo, plan[0][r], plan[4][r], 4)
+    ms, k = _groups(topo, core, to, 2)
+    g.wait_ge(sem.rin, kin)
+    g.remote_dma_fused([RemoteDMATransfer(dst_ids=[_dst(topo, d)], dma_engine_mask=ms[j], remote_sem=sem["x%d" % t],
+                                          src=T.rb[:, j * C:(j + 1) * C], dst=T.xw[:, t, :])
+                        for j, d in enumerate(to)], local_sem=sem.snt)
+    g.wait_ge(sem.snt, 2 * k)
+
+
+def _worker(g, core, T, topo, w, plan):
+    ranks, main, far, workers, relays, asend = plan
+    sem = T.sem
+    te, sc = g.tensor, g.scalar
+    tanh = ActivationFunctionType.Tanh
+
+    def xwait(t):
+        r = t // S
+        if r in main:
+            return sem["x%d" % (S * r)], _groups(topo, ranks[r], workers, W)[1]
+        q = (t % S) * 2 + w // 2
+        return sem["x%d" % t], _groups(topo, relays[r][q], [workers[2 * (w // 2)], workers[2 * (w // 2) + 1]], 2)[1]
+
+    a_from = [r for r in asend if core in asend[r]][0]
+    a_cnt = _groups(topo, ranks[a_from], workers, len(asend[a_from]))[1]
+    late = S * min(far) if far else -1
+
+    def bank(t):
+        o = (t % NBANK) * 512
+        return T.ps[:, o:o + C]
+
+    g.vector.memset(T.ones[:], 1.0).then_inc(sem.one, 1)
+    g.wait_ge(sem.one, 1)
+    g.affine_select(T.ident[:], T.ones[:], [[-1, 128]], AluOpType.is_equal, 0.0, 0, 1).then_inc(sem.idn, 1)
+
+    te.wait_ge(sem.idn, 1)
+    for t in range(1, NT):
+        xs_, xc = xwait(t)
+        if t == late:
+            te.wait_ge(sem["h%d" % (t - 1)], 1)
+            te.matmul(bank(t), T.asb[:], T.hb[:, t - 1, :], True, False)
+            te.wait_ge(xs_, xc)
+            te.matmul(bank(t), T.ident[:], T.xw[:, t, :], False, True).then_inc(sem["m%d" % t], 1)
+        else:
+            te.wait_ge(xs_, xc)
+            te.matmul(bank(t), T.ident[:], T.xw[:, t, :], True, False)
+            if t == 1:
+                te.wait_ge(sem.asem, a_cnt)
+            te.wait_ge(sem["h%d" % (t - 1)], 1)
+            te.matmul(bank(t), T.asb[:], T.hb[:, t - 1, :], False, True).then_inc(sem["m%d" % t], 1)
+
+    xs_, xc = xwait(0)
+    sc.wait_ge(xs_, xc)
+    sc.activation(T.hb[:, 0, :], T.xw[:, 0, :], tanh).then_inc(sem.h0, 1)
+    for t in range(1, NT):
+        sc.wait_ge(sem["m%d" % t], 1)
+        sc.activation(T.hb[:, t, :], bank(t), tanh).then_inc(sem["h%d" % t], 1)
+
+    order = list(range(N))
+    if w >= W // 2:
+        for i in range(N - 1, 2, -2):
+            order[i], order[i - 1] = order[i - 1], order[i]
+    sent = 0
+    for r in order:
+        rid, pid, _ = topo.addr(ranks[r])
+        m, k = _back_engines(topo, core, ranks[r])
+        if r in NAT:
+            for s in range(S):
+                g.wait_ge(sem["h%d" % (S * r + s)], 1)
+                g.remote_dma(out_ap=T.yn[:, s * B + w * C:s * B + (w + 1) * C], in_ap=T.hb[:, S * r + s, :],
+                             remote_sem=sem["y%d" % s], local_sem=sem.snt, pid=pid, routing_id=rid,
+                             dma_engine_mask=m)
+                sent += k
+        else:
+            for s in range(S):
+                g.wait_ge(sem["h%d" % (S * r + s)], 1)
+            g.remote_dma(out_ap=T.yl[:, w, :, :], in_ap=T.hb[:, S * r:S * r + S, :],
+                         remote_sem=sem.yp, local_sem=sem.snt, pid=pid, routing_id=rid, dma_engine_mask=m)
+            sent += k
+    g.wait_ge(sem.snt, sent)
+
+
+def rank_program(g, core, T, topo):
+    plan = _plan(T, topo)
+    r = T.rank_of(core)
+    if r is not None:
+        _rank(g, core, T, topo, r, plan)
+        return
+    if core in plan[3]:
+        _worker(g, core, T, topo, plan[3].index(core), plan)
+        return
+    for fr, rl in plan[4].items():
+        if core in rl:
+            _relay(g, core, T, topo, fr, rl.index(core), plan)
+            return

@@ -9,7 +9,6 @@ NBANK = 4
 NAT = (5, 6)
 
 SCRATCH = {
-    "xs": ("sbuf", [128, W, S, C], "bfloat16"),
     "xn": ("sbuf", [128, S * B], "bfloat16"),
     "asb": ("sbuf", [128, 128], "bfloat16"),
     "rb": ("sbuf", [128, 2 * C], "bfloat16"),
@@ -21,7 +20,7 @@ SCRATCH = {
     "yl": ("sbuf", [128, W, S, C], "bfloat16"),
     "yn": ("sbuf", [128, S * B], "bfloat16"),
 }
-SEMAPHORES = (["ld", "lda", "asem", "one", "idn", "snt", "rin", "yp", "y0", "y1", "st"]
+SEMAPHORES = (["ld0", "ld1", "lda", "asem", "one", "idn", "snt", "rin", "yp", "y0", "y1", "st"]
               + ["x%d" % t for t in range(NT)] + ["m%d" % t for t in range(NT)] + ["h%d" % t for t in range(NT)])
 
 
@@ -74,11 +73,11 @@ def _rank(g, core, T, topo, r, plan):
     ranks, main, far, workers, relays, asend = plan
     sem = T.sem
     sent = 0
+    g.sync.dma_start(T.xn[:, 0:B], T.x[:, 0:B]).then_inc(sem.ld0, 16)
+    if r in asend:
+        g.scalar.dma_start(T.asb[:], T.a[:]).then_inc(sem.lda, 16)
+    g.scalar.dma_start(T.xn[:, B:2 * B], T.x[:, B:2 * B]).then_inc(sem.ld1, 16)
     if r in main:
-        if r in asend:
-            g.scalar.dma_start(T.asb[:], T.a[:]).then_inc(sem.lda, 16)
-        g.sync.dma_start(T.xs[:, :, 0, :], T.x[:, 0:B]).then_inc(sem.ld, 16)
-        g.scalar.dma_start(T.xs[:, :, 1, :], T.x[:, B:2 * B]).then_inc(sem.ld, 16)
         if r in asend:
             to = asend[r]
             ms, k = _groups(topo, core, workers, len(to))
@@ -88,22 +87,25 @@ def _rank(g, core, T, topo, r, plan):
                                local_sem=sem.snt)
             sent += k * len(to)
         ms, k = _groups(topo, core, workers, W)
-        g.wait_ge(sem.ld, 32)
-        g.remote_dma_fused([RemoteDMATransfer(dst_ids=[_dst(topo, d)], dma_engine_mask=ms[w],
-                                              remote_sem=sem["x%d" % (S * r)],
-                                              src=T.xs[:, w, :, :], dst=T.xw[:, S * r:S * r + S, :])
-                            for w, d in enumerate(workers)], local_sem=sem.snt)
-        sent += k * W
+        for s in range(S):
+            t = S * r + s
+            g.wait_ge(sem["ld%d" % s], 16)
+            g.remote_dma_fused([RemoteDMATransfer(dst_ids=[_dst(topo, d)], dma_engine_mask=ms[w],
+                                                  remote_sem=sem["x%d" % t],
+                                                  src=T.xn[:, s * B + w * C:s * B + (w + 1) * C], dst=T.xw[:, t, :])
+                                for w, d in enumerate(workers)], local_sem=sem.snt)
+            sent += k * W
     else:
         rl = relays[r]
-        g.sync.dma_start(T.xn[:], T.x[:]).then_inc(sem.ld, 16)
-        ms, k = _groups(topo, core, rl, 4)
-        g.wait_ge(sem.ld, 16)
-        g.remote_dma_fused([RemoteDMATransfer(dst_ids=[_dst(topo, d)], dma_engine_mask=ms[q], remote_sem=sem.rin,
-                                              src=T.xn[:, q * 2 * C:(q + 1) * 2 * C], dst=T.rb[:])
-                            for q, d in enumerate(rl)], local_sem=sem.snt)
-        sent += k * 4
-    full = sum(_back_engines(topo, d, core)[1] for d in workers)
+        ms, k = _groups(topo, core, rl, 2)
+        for s in range(S):
+            g.wait_ge(sem["ld%d" % s], 16)
+            g.remote_dma_fused([RemoteDMATransfer(dst_ids=[_dst(topo, rl[2 * s + hf])], dma_engine_mask=ms[hf],
+                                                  remote_sem=sem.rin,
+                                                  src=T.xn[:, (2 * s + hf) * 2 * C:(2 * s + hf + 1) * 2 * C],
+                                                  dst=T.rb[:]) for hf in range(2)], local_sem=sem.snt)
+            sent += k * 2
+    full = sum(_groups(topo, d, ranks, 1)[1] for d in workers)
     if r in NAT:
         g.sync.wait_ge(sem.y0, full)
         g.sync.dma_start(T.y[:, 0:B], T.yn[:, 0:B]).then_inc(sem.st, 16)
@@ -118,18 +120,13 @@ def _rank(g, core, T, topo, r, plan):
     g.wait_ge(sem.st, 32)
 
 
-def _back_engines(topo, worker, rank_core):
-    e = _bits(topo.mask(worker, rank_core))[:8]
-    return sum(1 << b for b in e), len(e)
-
-
 def _relay(g, core, T, topo, r, q, plan):
     workers = plan[3]
     sem = T.sem
     s, hf = q // 2, q % 2
     t = S * r + s
     to = [workers[2 * hf], workers[2 * hf + 1]]
-    _, kin = _groups(topo, plan[0][r], plan[4][r], 4)
+    _, kin = _groups(topo, plan[0][r], plan[4][r], 2)
     ms, k = _groups(topo, core, to, 2)
     g.wait_ge(sem.rin, kin)
     g.remote_dma_fused([RemoteDMATransfer(dst_ids=[_dst(topo, d)], dma_engine_mask=ms[j], remote_sem=sem["x%d" % t],
@@ -147,7 +144,7 @@ def _worker(g, core, T, topo, w, plan):
     def xwait(t):
         r = t // S
         if r in main:
-            return sem["x%d" % (S * r)], _groups(topo, ranks[r], workers, W)[1]
+            return sem["x%d" % t], _groups(topo, ranks[r], workers, W)[1]
         q = (t % S) * 2 + w // 2
         return sem["x%d" % t], _groups(topo, relays[r][q], [workers[2 * (w // 2)], workers[2 * (w // 2) + 1]], 2)[1]
 
@@ -186,27 +183,23 @@ def _worker(g, core, T, topo, w, plan):
         sc.wait_ge(sem["m%d" % t], 1)
         sc.activation(T.hb[:, t, :], bank(t), tanh).then_inc(sem["h%d" % t], 1)
 
-    order = list(range(N))
-    if w >= W // 2:
-        for i in range(N - 1, 2, -2):
-            order[i], order[i - 1] = order[i - 1], order[i]
+    m1, k1 = _groups(topo, core, ranks, 1)
     sent = 0
-    for r in order:
+    for r in range(N):
         rid, pid, _ = topo.addr(ranks[r])
-        m, k = _back_engines(topo, core, ranks[r])
         if r in NAT:
             for s in range(S):
                 g.wait_ge(sem["h%d" % (S * r + s)], 1)
                 g.remote_dma(out_ap=T.yn[:, s * B + w * C:s * B + (w + 1) * C], in_ap=T.hb[:, S * r + s, :],
                              remote_sem=sem["y%d" % s], local_sem=sem.snt, pid=pid, routing_id=rid,
-                             dma_engine_mask=m)
-                sent += k
+                             dma_engine_mask=m1[0])
+                sent += k1
         else:
             for s in range(S):
                 g.wait_ge(sem["h%d" % (S * r + s)], 1)
             g.remote_dma(out_ap=T.yl[:, w, :, :], in_ap=T.hb[:, S * r:S * r + S, :],
-                         remote_sem=sem.yp, local_sem=sem.snt, pid=pid, routing_id=rid, dma_engine_mask=m)
-            sent += k
+                         remote_sem=sem.yp, local_sem=sem.snt, pid=pid, routing_id=rid, dma_engine_mask=m1[0])
+            sent += k1
     g.wait_ge(sem.snt, sent)
 
 

@@ -5,7 +5,9 @@ N, S, B = 7, 2, 512
 NT = N * S
 W = 4
 C = B // W
-NBANK = 4
+J = 2
+H = C // J
+NBANK = 8
 NAT = (5, 6)
 
 SCRATCH = {
@@ -21,7 +23,8 @@ SCRATCH = {
     "yn": ("sbuf", [128, S * B], "bfloat16"),
 }
 SEMAPHORES = (["ld0", "ld1", "lda", "asem", "one", "idn", "snt", "rin", "yp", "y0", "y1", "st"]
-              + ["x%d" % t for t in range(NT)] + ["m%d" % t for t in range(NT)] + ["h%d" % t for t in range(NT)])
+              + ["x%d" % t for t in range(NT)]
+              + ["%s%d" % (c, i) for c in "mh" for i in range(J * NT)])
 
 
 def _bits(mask):
@@ -152,36 +155,49 @@ def _worker(g, core, T, topo, w, plan):
     a_cnt = _groups(topo, ranks[a_from], workers, len(asend[a_from]))[1]
     late = S * min(far) if far else -1
 
-    def bank(t):
-        o = (t % NBANK) * 512
-        return T.ps[:, o:o + C]
+    def bank(t, j):
+        o = ((J * t + j) % NBANK) * 512
+        return T.ps[:, o:o + H]
+
+    def cols(buf, t, j):
+        return buf[:, t, j * H:(j + 1) * H]
 
     g.vector.memset(T.ones[:], 1.0).then_inc(sem.one, 1)
     g.wait_ge(sem.one, 1)
     g.affine_select(T.ident[:], T.ones[:], [[-1, 128]], AluOpType.is_equal, 0.0, 0, 1).then_inc(sem.idn, 1)
 
-    te.wait_ge(sem.idn, 1)
-    for t in range(1, NT):
-        xs_, xc = xwait(t)
-        if t == late:
-            te.wait_ge(sem["h%d" % (t - 1)], 1)
-            te.matmul(bank(t), T.asb[:], T.hb[:, t - 1, :], True, False)
-            te.wait_ge(xs_, xc)
-            te.matmul(bank(t), T.ident[:], T.xw[:, t, :], False, True).then_inc(sem["m%d" % t], 1)
-        else:
-            te.wait_ge(xs_, xc)
-            te.matmul(bank(t), T.ident[:], T.xw[:, t, :], True, False)
-            if t == 1:
-                te.wait_ge(sem.asem, a_cnt)
-            te.wait_ge(sem["h%d" % (t - 1)], 1)
-            te.matmul(bank(t), T.asb[:], T.hb[:, t - 1, :], False, True).then_inc(sem["m%d" % t], 1)
+    def put_x(t, first):
+        te.wait_ge(*xwait(t))
+        for j in range(J):
+            mm = te.matmul(bank(t, j), T.ident[:], cols(T.xw, t, j), first, not first)
+            if not first:
+                mm.then_inc(sem["m%d" % (J * t + j)], 1)
 
-    xs_, xc = xwait(0)
-    sc.wait_ge(xs_, xc)
-    sc.activation(T.hb[:, 0, :], T.xw[:, 0, :], tanh).then_inc(sem.h0, 1)
+    te.wait_ge(sem.idn, 1)
+    put_x(1, True)
+    te.wait_ge(sem.asem, a_cnt)
     for t in range(1, NT):
-        sc.wait_ge(sem["m%d" % t], 1)
-        sc.activation(T.hb[:, t, :], bank(t), tanh).then_inc(sem["h%d" % t], 1)
+        for j in range(J):
+            te.wait_ge(sem["h%d" % (J * (t - 1) + j)], 1)
+            mm = te.matmul(bank(t, j), T.asb[:], cols(T.hb, t - 1, j), t == late, t != late)
+            if t != late:
+                mm.then_inc(sem["m%d" % (J * t + j)], 1)
+        if t == late:
+            put_x(t, False)
+        if t + 1 < NT and t + 1 != late:
+            put_x(t + 1, True)
+
+    sc.wait_ge(*xwait(0))
+    for j in range(J):
+        sc.activation(cols(T.hb, 0, j), cols(T.xw, 0, j), tanh).then_inc(sem["h%d" % j], 1)
+    for t in range(1, NT):
+        for j in range(J):
+            sc.wait_ge(sem["m%d" % (J * t + j)], 1)
+            sc.activation(cols(T.hb, t, j), bank(t, j), tanh).then_inc(sem["h%d" % (J * t + j)], 1)
+
+    def ready(t):
+        for j in range(J):
+            g.wait_ge(sem["h%d" % (J * t + j)], 1)
 
     m1, k1 = _groups(topo, core, ranks, 1)
     sent = 0
@@ -189,14 +205,14 @@ def _worker(g, core, T, topo, w, plan):
         rid, pid, _ = topo.addr(ranks[r])
         if r in NAT:
             for s in range(S):
-                g.wait_ge(sem["h%d" % (S * r + s)], 1)
+                ready(S * r + s)
                 g.remote_dma(out_ap=T.yn[:, s * B + w * C:s * B + (w + 1) * C], in_ap=T.hb[:, S * r + s, :],
                              remote_sem=sem["y%d" % s], local_sem=sem.snt, pid=pid, routing_id=rid,
                              dma_engine_mask=m1[0])
                 sent += k1
         else:
             for s in range(S):
-                g.wait_ge(sem["h%d" % (S * r + s)], 1)
+                ready(S * r + s)
             g.remote_dma(out_ap=T.yl[:, w, :, :], in_ap=T.hb[:, S * r:S * r + S, :],
                          remote_sem=sem.yp, local_sem=sem.snt, pid=pid, routing_id=rid, dma_engine_mask=m1[0])
             sent += k1

from concourse.bass import DstId, RemoteDMATransfer
from concourse.mybir import AluOpType, ActivationFunctionType

N, S, B = 7, 2, 512
NT = N * S
W = 4
C = B // W
J = 2
H = C // J
NBANK = 8
NAT = (5, 6)

SCRATCH = {
    "xn": ("sbuf", [128, S * B], "bfloat16"),
    "asb": ("sbuf", [128, 128], "bfloat16"),
    "rb": ("sbuf", [128, 2 * C], "bfloat16"),
    "xw": ("sbuf", [128, NT, C], "bfloat16"),
    "hb": ("sbuf", [128, NT, C], "bfloat16"),
    "ones": ("sbuf", [128, 128], "bfloat16"),
    "ident": ("sbuf", [128, 128], "bfloat16"),
    "ps": ("psum", [128, NBANK * 512], "float32"),
    "yl": ("sbuf", [128, W, S, C], "bfloat16"),
    "yn": ("sbuf", [128, S * B], "bfloat16"),
}
SEMAPHORES = (["ld0", "ld1", "lda", "asem", "one", "idn", "snt", "rin", "yp", "y0", "y1", "st"]
              + ["x%d" % t for t in range(NT)]
              + ["%s%d" % (c, i) for c in "mh" for i in range(J * NT)])


def _bits(mask):
    return [i for i in range(16) if (mask >> i) & 1]


def _groups(topo, src, dsts, n):
    m = topo.mask(src, dsts[0])
    for d in dsts[1:]:
        m &= topo.mask(src, d)
    e = _bits(m)
    k = len(e) // n
    return [sum(1 << b for b in e[i * k:(i + 1) * k]) for i in range(n)], k


def _plan(T, topo):
    ranks = list(T.cores)
    chips = [topo.chip(c) for c in ranks]

    def near(a, b):
        return a == b or topo.same_plane(a, b)
    best = max(chips, key=lambda c: sum(1 for d in chips if near(c, d)))
    main = [r for r in range(N) if near(chips[r], best)]
    far = [r for r in range(N) if r not in main]
    allc = list(range(topo.CHIPS * topo.CORES_PER_CHIP))
    free = [c for c in range(topo.CHIPS) if near(c, best) and c not in chips]
    wchips = (free + [chips[r] for r in main])[:W]
    die0 = topo.die(ranks[0])
    workers = []
    for w, ch in enumerate(wchips):
        cand = [c for c in allc if topo.chip(c) == ch and c not in ranks
                and all(topo.may_write(c, q) for q in ranks)]
        want = [c for c in cand if (topo.die(c) == die0) == (w % 2 == 0)]
        workers.append((want or cand)[0])
    relays = {}
    for r in far:
        relays[r] = [c for c in allc if topo.chip(c) == chips[r] and c != ranks[r]
                     and all(topo.may_write(c, q) for q in workers)][:4]
    asend = {main[-1]: workers[:W // 2], main[-2]: workers[W // 2:]}
    return ranks, main, far, workers, relays, asend


def _dst(topo, c):
    rid, pid, _ = topo.addr(c)
    return DstId(rid=rid, pnc=pid)


def _rank(g, core, T, topo, r, plan):
    ranks, main, far, workers, relays, asend = plan
    sem = T.sem
    sent = 0
    g.sync.dma_start(T.xn[:, 0:B], T.x[:, 0:B]).then_inc(sem.ld0, 16)
    if r in asend:
        g.scalar.dma_start(T.asb[:], T.a[:]).then_inc(sem.lda, 16)
    g.scalar.dma_start(T.xn[:, B:2 * B], T.x[:, B:2 * B]).then_inc(sem.ld1, 16)
    if r in main:
        if r in asend:
            to = asend[r]
            ms, k = _groups(topo, core, workers, len(to))
            g.wait_ge(sem.lda, 16)
            g.remote_dma_fused([RemoteDMATransfer(dst_ids=[_dst(topo, d)], dma_engine_mask=ms[i], remote_sem=sem.asem,
                                                  src=T.asb[:], dst=T.asb[:]) for i, d in enumerate(to)],
                               local_sem=sem.snt)
            sent += k * len(to)
        ms, k = _groups(topo, core, workers, W)
        for s in range(S):
            t = S * r + s
            g.wait_ge(sem["ld%d" % s], 16)
            g.remote_dma_fused([RemoteDMATransfer(dst_ids=[_dst(topo, d)], dma_engine_mask=ms[w],
                                                  remote_sem=sem["x%d" % t],
                                                  src=T.xn[:, s * B + w * C:s * B + (w + 1) * C], dst=T.xw[:, t, :])
                                for w, d in enumerate(workers)], local_sem=sem.snt)
            sent += k * W
    else:
        rl = relays[r]
        ms, k = _groups(topo, core, rl, 2)
        for s in range(S):
            g.wait_ge(sem["ld%d" % s], 16)
            g.remote_dma_fused([RemoteDMATransfer(dst_ids=[_dst(topo, rl[2 * s + hf])], dma_engine_mask=ms[hf],
                                                  remote_sem=sem.rin,
                                                  src=T.xn[:, (2 * s + hf) * 2 * C:(2 * s + hf + 1) * 2 * C],
                                                  dst=T.rb[:]) for hf in range(2)], local_sem=sem.snt)
            sent += k * 2
    full = sum(_groups(topo, d, ranks, 1)[1] for d in workers)
    if r in NAT:
        g.sync.wait_ge(sem.y0, full)
        g.sync.dma_start(T.y[:, 0:B], T.yn[:, 0:B]).then_inc(sem.st, 16)
        g.scalar.wait_ge(sem.y1, full)
        g.scalar.dma_start(T.y[:, B:2 * B], T.yn[:, B:2 * B]).then_inc(sem.st, 16)
    else:
        g.sync.wait_ge(sem.yp, full)
        g.sync.dma_start(T.y[:, 0:B], T.yl[:, :, 0, :]).then_inc(sem.st, 16)
        g.scalar.wait_ge(sem.yp, full)
        g.scalar.dma_start(T.y[:, B:2 * B], T.yl[:, :, 1, :]).then_inc(sem.st, 16)
    g.wait_ge(sem.snt, sent)
    g.wait_ge(sem.st, 32)


def _relay(g, core, T, topo, r, q, plan):
    workers = plan[3]
    sem = T.sem
    s, hf = q // 2, q % 2
    t = S * r + s
    to = [workers[2 * hf], workers[2 * hf + 1]]
    _, kin = _groups(topo, plan[0][r], plan[4][r], 2)
    ms, k = _groups(topo, core, to, 2)
    g.wait_ge(sem.rin, kin)
    g.remote_dma_fused([RemoteDMATransfer(dst_ids=[_dst(topo, d)], dma_engine_mask=ms[j], remote_sem=sem["x%d" % t],
                                          src=T.rb[:, j * C:(j + 1) * C], dst=T.xw[:, t, :])
                        for j, d in enumerate(to)], local_sem=sem.snt)
    g.wait_ge(sem.snt, 2 * k)


def _worker(g, core, T, topo, w, plan):
    ranks, main, far, workers, relays, asend = plan
    sem = T.sem
    te, sc = g.tensor, g.scalar
    tanh = ActivationFunctionType.Tanh

    def xwait(t):
        r = t // S
        if r in main:
            return sem["x%d" % t], _groups(topo, ranks[r], workers, W)[1]
        q = (t % S) * 2 + w // 2
        return sem["x%d" % t], _groups(topo, relays[r][q], [workers[2 * (w // 2)], workers[2 * (w // 2) + 1]], 2)[1]

    a_from = [r for r in asend if core in asend[r]][0]
    a_cnt = _groups(topo, ranks[a_from], workers, len(asend[a_from]))[1]
    late = S * min(far) if far else -1

    def bank(t, j):
        o = ((J * t + j) % NBANK) * 512
        return T.ps[:, o:o + H]

    def cols(buf, t, j):
        return buf[:, t, j * H:(j + 1) * H]

    g.vector.memset(T.ones[:], 1.0).then_inc(sem.one, 1)
    g.wait_ge(sem.one, 1)
    g.affine_select(T.ident[:], T.ones[:], [[-1, 128]], AluOpType.is_equal, 0.0, 0, 1).then_inc(sem.idn, 1)

    def put_x(t, first):
        te.wait_ge(*xwait(t))
        for j in range(J):
            mm = te.matmul(bank(t, j), T.ident[:], cols(T.xw, t, j), first, not first)
            if not first:
                mm.then_inc(sem["m%d" % (J * t + j)], 1)

    te.wait_ge(sem.idn, 1)
    put_x(1, True)
    te.wait_ge(sem.asem, a_cnt)
    for t in range(1, NT):
        for j in range(J):
            te.wait_ge(sem["h%d" % (J * (t - 1) + j)], 1)
            mm = te.matmul(bank(t, j), T.asb[:], cols(T.hb, t - 1, j), t == late, t != late)
            if t != late:
                mm.then_inc(sem["m%d" % (J * t + j)], 1)
        if t == late:
            put_x(t, False)
        if t + 1 < NT and t + 1 != late:
            put_x(t + 1, True)

    sc.wait_ge(*xwait(0))
    for j in range(J):
        sc.activation(cols(T.hb, 0, j), cols(T.xw, 0, j), tanh).then_inc(sem["h%d" % j], 1)
    for t in range(1, NT):
        for j in range(J):
            sc.wait_ge(sem["m%d" % (J * t + j)], 1)
            sc.activation(cols(T.hb, t, j), bank(t, j), tanh).then_inc(sem["h%d" % (J * t + j)], 1)

    def ready(t):
        for j in range(J):
            g.wait_ge(sem["h%d" % (J * t + j)], 1)

    m1, k1 = _groups(topo, core, ranks, 1)
    sent = 0
    for r in range(N):
        rid, pid, _ = topo.addr(ranks[r])
        if r in NAT:
            for s in range(S):
                ready(S * r + s)
                g.remote_dma(out_ap=T.yn[:, s * B + w * C:s * B + (w + 1) * C], in_ap=T.hb[:, S * r + s, :],
                             remote_sem=sem["y%d" % s], local_sem=sem.snt, pid=pid, routing_id=rid,
                             dma_engine_mask=m1[0])
                sent += k1
        else:
            for s in range(S):
                ready(S * r + s)
            g.remote_dma(out_ap=T.yl[:, w, :, :], in_ap=T.hb[:, S * r:S * r + S, :],
                         remote_sem=sem.yp, local_sem=sem.snt, pid=pid, routing_id=rid, dma_engine_mask=m1[0])
            sent += k1
    g.wait_ge(sem.snt, sent)


def rank_program(g, core, T, topo):
    plan = _plan(T, topo)
    r = T.rank_of(core)
    if r is not None:
        _rank(g, core, T, topo, r, plan)
        return
    if core in plan[3]:
        _worker(g, core, T, topo, plan[3].index(core), plan)
        return
    for fr, rl in plan[4].items():
        if core in rl:
            _relay(g, core, T, topo, fr, rl.index(core), plan)
            return
